import numpy as np
import ml_dtypes


def mxq(x, axis, fmt="e4m3"):
    dtype, down = {"e4m3": (ml_dtypes.float8_e4m3fn, 7), "e5m2": (ml_dtypes.float8_e5m2, 14)}[fmt]
    v = np.moveaxis(np.asarray(x, np.float32).astype(ml_dtypes.bfloat16).astype(np.float64), axis, -1)
    blocks = v.reshape(v.shape[:-1] + (-1, 32))
    amax = np.abs(blocks).max(-1, keepdims=True)
    byte = np.maximum(np.where(amax > 0, np.frexp(amax)[1] - 1 + 127, 0) - down, 1)
    scale = np.exp2(byte - 127.0)
    codes = (blocks / scale).astype(np.float32).astype(dtype).astype(np.float64)
    return np.moveaxis((codes * scale).reshape(v.shape), -1, axis)


WIDE = False


def mx_kscale(k):
    if not WIDE:
        return np.ones(k)
    levels = np.array([10, -10, 5, -5, 0])
    if k % 512:
        return np.exp2(np.random.permutation(np.resize(levels, k // 32))).repeat(32)
    a = np.empty((k // 512, 16))
    for p in range(k // 512):
        a[p, :8] = np.random.permutation(np.resize(levels, 8))
        for g in range(8):
            far = levels[np.abs(levels - a[p, g]) >= 10]
            a[p, g + 8] = far[np.random.randint(len(far))]
    return np.exp2(a.ravel()).repeat(32)


def f64(x):
    return np.asarray(x).astype(np.float64)


def striped(idx):
    return np.tile(idx.reshape(-1, 16).T, (8, 1)).astype(np.uint16)


def unstriped(offs):
    return offs[:16].T.reshape(-1).astype(np.int64)


E2M1 = np.array([0.0, 0.5, 1.0, 1.5, 2.0, 3.0, 4.0, 6.0, -0.0, -0.5, -1.0, -1.5, -2.0, -3.0, -4.0, -6.0])


def pack_weight(w, fmt):
    k, n = w.shape
    w = f64(np.asarray(w, np.float32).astype(ml_dtypes.bfloat16)).reshape(k // 32, 32, n)
    amax = np.abs(w).max(1)
    if fmt == "e4m3":
        byte = np.frexp(amax)[1] - 1 + 127 - 7
    else:
        mant, ex = np.frexp(amax / 6.0)
        byte = np.where(mant > 0.5, ex, ex - 1) + 127
    byte = np.clip(np.where(amax > 0, byte, 1), 1, 254)
    scaled = (w * np.exp2(127.0 - byte)[:, None, :]).reshape(k, n).astype(np.float32)
    by_word = np.ascontiguousarray(scaled.reshape(k // 512, 128, 4, n).transpose(0, 1, 3, 2))
    if fmt == "e4m3":
        words = by_word.astype(ml_dtypes.float8_e4m3fn).view(np.uint8)
    else:
        c = by_word.astype(ml_dtypes.float4_e2m1fn).view(np.uint8) & 0xF
        words = (c[..., 0::2] | (c[..., 1::2] << 4)).reshape(k // 512, 128, 2 * n)
    return np.ascontiguousarray(words), np.ascontiguousarray(byte.astype(np.uint8).reshape(k // 512, 16, n))


def unpack_weight(words, scales, fmt):
    g, _, n = scales.shape
    words = np.ascontiguousarray(words).reshape(g, 128, n, -1)
    if fmt == "e4m3":
        vals = words.view(ml_dtypes.float8_e4m3fn).astype(np.float64)
    else:
        nib = np.empty((g, 128, n, 4), np.uint8)
        nib[..., 0::2] = words & 0xF
        nib[..., 1::2] = words >> 4
        vals = E2M1[nib]
    vals = vals * np.repeat(np.exp2(scales.astype(np.float64) - 127.0), 8, axis=1)[..., None]
    return vals.transpose(0, 1, 3, 2).reshape(g * 512, n)


def d_silu(v):
    s = 1.0 / (1.0 + np.exp(-np.maximum(v, -700.0)))
    return s * (1.0 + v * (1.0 - s))


K, T, E1, C1, E2, C2, H = 512, 768, 3, 256, 6, 128, 512
N = 1024


def by_expert(wq, xq, E, C):
    return np.concatenate([wq[e].T @ xq[:, e * C:(e + 1) * C] for e in range(E)], axis=1)


def setup_inputs():
    n = np.random.standard_normal
    v = mx_kscale(N)
    u = mx_kscale(H)
    slots1, slots2 = np.random.permutation(T), np.random.permutation(T)
    dy = pack_weight(n((N, T)) * v[:, None], "e4m3")
    return {
        "dy_words": dy[0],
        "dy_scales": dy[1],
        "w2t": (n((E2, N, H)) / np.sqrt(N) / v[None, :, None] * u).astype(np.float32),
        "w1t": (n((E1, H, K)) / np.sqrt(H) / u[None, :, None]).astype(np.float32),
        "a": (n((H, T))).astype(np.float32),
        "gate1": (np.tile(np.random.uniform(0.2, 1.0, T), (128, 1))).astype(np.float32),
        "gate2": (np.tile(np.random.uniform(0.2, 1.0, T), (128, 1))).astype(np.float32),
        "offs": striped(slots1),
        "offs2": striped(slots2),
    }


def reference(dy_words, dy_scales, w2t, w1t, a, gate1, gate2, offs, offs2):
    w2tq = mxq(f64(w2t), 1, "e4m3")
    w1tq = mxq(f64(w1t), 1, "e4m3")
    idx, idx2 = unstriped(offs), unstriped(offs2)
    gq = unpack_weight(dy_words, dy_scales, "e4m3")[:, idx2]
    dc = np.zeros((H, T))
    dc[:, idx2] = f64(gate2[:1]) * by_expert(w2tq, gq, E2, C2)
    da = f64(gate1[:1]) * dc[:, idx] * d_silu(f64(a))
    out = np.zeros((K, T))
    out[:, idx] = by_expert(w1tq, mxq(da, 0, "e4m3"), E1, C1)
    return out

@@ -1,0 +1,207 @@
+from contextlib import ExitStack
+
+import concourse.mybir as mybir
+
+K, T, H, N = 512, 768, 512, 1024
+E1, C1 = 3, 256
+E2, C2 = 6, 128
+FLOPS = 2 * T * (N * H + H * K)
+
+F32 = mybir.dt.float32
+BF16 = mybir.dt.bfloat16
+I32 = mybir.dt.int32
+U32 = mybir.dt.uint32
+U16 = mybir.dt.uint16
+U8 = mybir.dt.uint8
+FP8X4 = mybir.dt.float8_e4m3fn_x4
+ACT = mybir.ActivationFunctionType
+ALU = mybir.AluOpType
+
+P = 128
+PACK = 4
+K_PASS = P * PACK
+PASSES = N // K_PASS
+RUN = 2
+LIST_ROWS = 16
+GATHER2 = 256
+
+
+def tile_moe_seb_silu_kernel(tc, dy_words, dy_scales, w2t, w1t, a, gate1, gate2, offs, offs2, out):
+    nc = tc.nc
+    with ExitStack() as ctx:
+        keep = ctx.enter_context(tc.tile_pool(name="keep", bufs=1))
+        raws = ctx.enter_context(tc.tile_pool(name="raws", bufs=8))
+        ring = ctx.enter_context(tc.tile_pool(name="ring", bufs=3))
+        codes2 = ctx.enter_context(tc.tile_pool(name="codes2", bufs=6))
+        psum = ctx.enter_context(tc.psum_pool(name="psum", bufs=4))
+
+        list1 = keep.tile([P, T // LIST_ROWS], U16, name="list1")
+        list2 = keep.tile([P, T // LIST_ROWS], U16, name="list2")
+        dy_in = [keep.tile([P, T], I32, name=f"dy_in{s}", align_bytes=64) for s in range(PASSES)]
+        dy_in_scales = keep.tile([P, T], U8, name="dy_in_scales", align_bytes=64)
+        dy_slots = [keep.tile([P, T], U32, name=f"dy_slots{s}", align_bytes=64) for s in range(PASSES)]
+        dy_slot_scales = keep.tile([P, T], U8, name="dy_slot_scales", align_bytes=64)
+        g1 = keep.tile([P, T], F32, name="g1")
+        g2 = keep.tile([P, T], F32, name="g2")
+        pre = keep.tile([P, PACK, T], F32, name="pre")
+        factor = keep.tile([P, PACK, T], F32, name="factor")
+        dc = [keep.tile([P, T], F32, name=f"dc{t}") for t in range(PACK)]
+        dx = [keep.tile([P, T], F32, name=f"dx{m}") for m in range(K // P)]
+
+        def entries(lst, first, count):
+            return lst[:, first // LIST_ROWS : (first + count) // LIST_ROWS]
+
+        def load_w2(f, s):
+            raw = raws.tile([P, PACK, H], F32, name="raw")
+            nc.sync.dma_start(out=raw[:], in_=w2t[f, s * K_PASS : (s + 1) * K_PASS, :].rearrange("(p j) c -> p j c", j=PACK))
+            return raw
+
+        def load_hidden_rows(dst, src):
+            rows = src.rearrange("(g t r) c -> r g t c", t=PACK, r=RUN)
+            for r in range(RUN):
+                nc.sync.dma_start(out=dst[r:P:RUN, :, :], in_=rows[r])
+
+        def load_w1(e):
+            raw = raws.tile([P, PACK, K], F32, name="raw")
+            load_hidden_rows(raw, w1t[e])
+            return raw
+
+        def quantize(pool, tag, grouped, width):
+            codes = pool.tile([P, width], U32, name=tag + "_codes", align_bytes=64)
+            scales = pool.tile([P, width], U8, name=tag + "_scales", align_bytes=64)
+            nc.vector.quantize_mx(out=codes[:].bitcast(FP8X4), scales=scales[:], in_=grouped[:])
+            return codes, scales
+
+        def group_w2(raw, on_vector):
+            grouped = ring.tile([P, PACK * H], BF16, name="grouped", align_bytes=64)
+            dst = grouped[:].rearrange("p (t g r j) -> p g t j r", t=PACK, r=RUN, j=PACK)
+            src = raw[:].rearrange("p j (g t r) -> p g t j r", t=PACK, r=RUN)
+            if on_vector:
+                nc.vector.tensor_copy(out=dst, in_=src)
+            else:
+                nc.scalar.copy(out=dst, in_=src)
+            return grouped
+
+        def group_plain(raw, width, tag):
+            grouped = ring.tile([P, PACK * width], BF16, name=tag, align_bytes=64)
+            nc.scalar.copy(
+                out=grouped[:].rearrange("p (c r t) -> p c t r", r=RUN, t=PACK),
+                in_=raw[:].rearrange("p t (c r) -> p c t r", r=RUN),
+            )
+            return grouped
+
+        nc.vector.memset(dy_in_scales[:].bitcast(I32), 0)
+        nc.sync.dma_start(list2[:], offs2)
+        for s in range(PASSES):
+            nc.sync.dma_start(out=dy_in[s][:], in_=dy_words[s].rearrange("p t d -> p (t d)").bitcast(I32))
+        raw2 = {(0, 0): load_w2(0, 0)}
+        for q in range(4):
+            nc.sync.dma_start(
+                out=dy_in_scales[32 * q : 32 * q + 4 * PASSES, :].bitcast(I32),
+                in_=dy_scales[:, 4 * q : 4 * q + 4, :].bitcast(I32),
+            )
+        raw2[0, 1] = load_w2(0, 1)
+        nc.sync.dma_start(out=g2[:], in_=gate2)
+        for s in range(PASSES):
+            raw2[1, s] = load_w2(1, s)
+        load_hidden_rows(pre, a)
+        nc.sync.dma_start(out=g1[:], in_=gate1)
+        nc.sync.dma_start(list1[:], offs)
+
+        for first in range(0, T, GATHER2):
+            cols = slice(first, first + GATHER2)
+            which = entries(list2, first, GATHER2)
+            for s in range(PASSES):
+                nc.vector.tensor_copy(dy_slots[s][:, cols], dy_in[s][:].bitcast(U32).indirect(which))
+            nc.vector.tensor_copy(dy_slot_scales[:, cols], dy_in_scales[:].indirect(which))
+
+        def second_layer(f):
+            cols = slice(f * C2, (f + 1) * C2)
+            w = [quantize(codes2, "w2", group_w2(raw2[f, s], (f, s) == (0, 1)), H) for s in range(PASSES)]
+            acc = psum.tile([P, PACK, C2], F32, name="acc2")
+            for t in range(PACK):
+                w_cols = slice(t * P, (t + 1) * P)
+                for s in range(PASSES):
+                    nc.tensor.matmul_mx(
+                        out=acc[:, t, :],
+                        lhsT=w[s][0][:, w_cols].bitcast(FP8X4),
+                        lhsT_scale=w[s][1][:, w_cols],
+                        rhs=dy_slots[s][:, cols].bitcast(FP8X4),
+                        rhs_scale=dy_slot_scales[4 * s : P, cols],
+                        start=(s == 0),
+                        stop=(s == PASSES - 1),
+                    )
+            sums = ring.tile([P, PACK, C2], F32, name="sums2")
+            nc.scalar.copy(out=sums[:], in_=acc[:])
+            for t in range(PACK):
+                nc.vector.tensor_tensor(
+                    dc[t][:].indirect(entries(list2, f * C2, C2)), sums[:, t, :], g2[:, cols], ALU.mult
+                )
+
+        def silu_parts():
+            for t in range(PACK):
+                nc.scalar.activation(out=factor[:, t, :], in_=pre[:, t, :], func=ACT.Silu, scale=-1.0)
+
+        def make_factor(e):
+            cols = slice(e * C1, (e + 1) * C1)
+            nc.scalar.activation(out=pre[:, :, cols], in_=pre[:, :, cols], func=ACT.Sigmoid)
+            nc.vector.scalar_tensor_tensor(
+                out=factor[:, :, cols], in0=factor[:, :, cols], scalar=1.0, in1=pre[:, :, cols],
+                op0=ALU.subtract, op1=ALU.mult,
+            )
+            nc.vector.scalar_tensor_tensor(
+                out=factor[:, :, cols], in0=factor[:, :, cols], scalar=-1.0,
+                in1=g1[:, cols].unsqueeze(1).to_broadcast([P, PACK, C1]),
+                op0=ALU.mult, op1=ALU.mult,
+            )
+
+        raw1 = {}
+        for f in range(E2):
+            if f + 2 < E2:
+                for s in range(PASSES):
+                    raw2[f + 2, s] = load_w2(f + 2, s)
+            second_layer(f)
+            if f == 1:
+                silu_parts()
+            if 2 <= f < 2 + E1:
+                make_factor(f - 2)
+        for e in range(E1):
+            raw1[e] = load_w1(e)
+        w1q = [quantize(keep, f"w1_{e}", group_plain(raw1[e], K, "grouped"), K) for e in range(E1)]
+
+        def gather_da(e):
+            cols = slice(e * C1, (e + 1) * C1)
+            da = ring.tile([P, PACK, C1], F32, name="da")
+            for t in range(PACK):
+                nc.vector.tensor_tensor(
+                    da[:, t, :], dc[t][:].indirect(entries(list1, e * C1, C1)), factor[:, t, cols], ALU.mult
+                )
+            return group_plain(da, C1, "da_grouped")
+
+        def first_layer(e, grouped):
+            da_codes, da_scales = quantize(ring, "da", grouped, C1)
+            sums = ring.tile([P, K // P, C1], F32, name="sums1")
+            for half in range(2):
+                acc = psum.tile([P, 2, C1], F32, name="acc1")
+                for u in range(2):
+                    m = 2 * half + u
+                    w_cols = slice(m * P, (m + 1) * P)
+                    nc.tensor.matmul_mx(
+                        out=acc[:, u, :],
+                        lhsT=w1q[e][0][:, w_cols].bitcast(FP8X4),
+                        lhsT_scale=w1q[e][1][:, w_cols],
+                        rhs=da_codes[:].bitcast(FP8X4),
+                        rhs_scale=da_scales[:],
+                        start=True,
+                        stop=True,
+                    )
+                nc.scalar.copy(out=sums[:, 2 * half : 2 * half + 2, :], in_=acc[:])
+            return sums
+
+        groups = [gather_da(e) for e in range(E1)]
+        results = [first_layer(e, groups[e]) for e in range(E1)]
+        for e in range(E1):
+            for m in range(K // P):
+                nc.vector.tensor_copy(dx[m][:].indirect(entries(list1, e * C1, C1)), results[e][:, m, :])
+        for m in range(K // P):
+            nc.sync.dma_start(out=out[m * P : (m + 1) * P, :], in_=dx[m][:])

@@ -30,7 +30,7 @@ def tile_moe_seb_silu_kernel(tc, dy_words, dy_scales, w2t, w1t, a, gate1, gate2,
     nc = tc.nc
     with ExitStack() as ctx:
         keep = ctx.enter_context(tc.tile_pool(name="keep", bufs=1))
-        raws = ctx.enter_context(tc.tile_pool(name="raws", bufs=8))
+        raws = ctx.enter_context(tc.tile_pool(name="raws", bufs=9))
         ring = ctx.enter_context(tc.tile_pool(name="ring", bufs=3))
         codes2 = ctx.enter_context(tc.tile_pool(name="codes2", bufs=6))
         psum = ctx.enter_context(tc.psum_pool(name="psum", bufs=4))
@@ -90,6 +90,9 @@ def tile_moe_seb_silu_kernel(tc, dy_words, dy_scales, w2t, w1t, a, gate1, gate2,
             )
             return grouped
 
+        warm = keep.tile([P, 2], F32, name="warm")
+        nc.gpsimd.memset(warm[:, 0:1], 0.0)
+        nc.scalar.activation(out=warm[:, 1:2], in_=warm[:, 0:1], func=ACT.Silu)
         nc.vector.memset(dy_in_scales[:].bitcast(I32), 0)
         nc.sync.dma_start(list2[:], offs2)
         for s in range(PASSES):
@@ -102,22 +105,24 @@ def tile_moe_seb_silu_kernel(tc, dy_words, dy_scales, w2t, w1t, a, gate1, gate2,
             )
         raw2[0, 1] = load_w2(0, 1)
         nc.sync.dma_start(out=g2[:], in_=gate2)
-        for s in range(PASSES):
-            raw2[1, s] = load_w2(1, s)
         load_hidden_rows(pre, a)
         nc.sync.dma_start(out=g1[:], in_=gate1)
         nc.sync.dma_start(list1[:], offs)
+        for s in range(PASSES):
+            raw2[1, s] = load_w2(1, s)
 
-        for first in range(0, T, GATHER2):
-            cols = slice(first, first + GATHER2)
-            which = entries(list2, first, GATHER2)
+        for first, count in ((0, GATHER2), (GATHER2, T - GATHER2)):
+            cols = slice(first, first + count)
+            which = entries(list2, first, count)
             for s in range(PASSES):
                 nc.vector.tensor_copy(dy_slots[s][:, cols], dy_in[s][:].bitcast(U32).indirect(which))
             nc.vector.tensor_copy(dy_slot_scales[:, cols], dy_in_scales[:].indirect(which))
 
-        def second_layer(f):
+        def second_weights(f):
+            return [quantize(codes2, "w2", group_w2(raw2[f, s], f == 1), H) for s in range(PASSES)]
+
+        def second_layer(f, w):
             cols = slice(f * C2, (f + 1) * C2)
-            w = [quantize(codes2, "w2", group_w2(raw2[f, s], (f, s) == (0, 1)), H) for s in range(PASSES)]
             acc = psum.tile([P, PACK, C2], F32, name="acc2")
             for t in range(PACK):
                 w_cols = slice(t * P, (t + 1) * P)
@@ -131,8 +136,11 @@ def tile_moe_seb_silu_kernel(tc, dy_words, dy_scales, w2t, w1t, a, gate1, gate2,
                         start=(s == 0),
                         stop=(s == PASSES - 1),
                     )
-            sums = ring.tile([P, PACK, C2], F32, name="sums2")
-            nc.scalar.copy(out=sums[:], in_=acc[:])
+            return acc
+
+        def scatter_dc(f, acc, sums):
+            cols = slice(f * C2, (f + 1) * C2)
+            nc.scalar.copy(out=sums, in_=acc[:])
             for t in range(PACK):
                 nc.vector.tensor_tensor(
                     dc[t][:].indirect(entries(list2, f * C2, C2)), sums[:, t, :], g2[:, cols], ALU.mult
@@ -160,11 +168,17 @@ def tile_moe_seb_silu_kernel(tc, dy_words, dy_scales, w2t, w1t, a, gate1, gate2,
             if f + 2 < E2:
                 for s in range(PASSES):
                     raw2[f + 2, s] = load_w2(f + 2, s)
-            second_layer(f)
-            if f == 1:
+            w = second_weights(f)
+            if f >= 2:
+                scatter_dc(f - 1, acc, raw2[f, 1][:, 0, :].rearrange("p (t c) -> p t c", t=PACK))
+            acc = second_layer(f, w)
+            if f in (0, E2 - 1):
+                scatter_dc(f, acc, keep.tile([P, PACK, C2], F32, name="sums2")[:])
+            if f == 0:
                 silu_parts()
-            if 2 <= f < 2 + E1:
-                make_factor(f - 2)
+            if f == 1:
+                for e in range(E1):
+                    make_factor(e)
         for e in range(E1):
             raw1[e] = load_w1(e)
         w1q = [quantize(keep, f"w1_{e}", group_plain(raw1[e], K, "grouped"), K) for e in range(E1)]
@@ -180,7 +194,10 @@ def tile_moe_seb_silu_kernel(tc, dy_words, dy_scales, w2t, w1t, a, gate1, gate2,
 
         def first_layer(e, grouped):
             da_codes, da_scales = quantize(ring, "da", grouped, C1)
-            sums = ring.tile([P, K // P, C1], F32, name="sums1")
+            if e + 1 < E1:
+                sums = raw1[e + 1][:, 0:2, :].rearrange("p j (u c) -> p (j u) c", c=C1)
+            else:
+                sums = keep.tile([P, K // P, C1], F32, name="sums1")[:]
             for half in range(2):
                 acc = psum.tile([P, 2, C1], F32, name="acc1")
                 for u in range(2):
@@ -198,8 +215,12 @@ def tile_moe_seb_silu_kernel(tc, dy_words, dy_scales, w2t, w1t, a, gate1, gate2,
                 nc.scalar.copy(out=sums[:, 2 * half : 2 * half + 2, :], in_=acc[:])
             return sums
 
-        groups = [gather_da(e) for e in range(E1)]
-        results = [first_layer(e, groups[e]) for e in range(E1)]
+        groups = [gather_da(0)]
+        results = []
+        for e in range(E1):
+            if e + 1 < E1:
+                groups.append(gather_da(e + 1))
+            results.append(first_layer(e, groups[e]))
         for e in range(E1):
             for m in range(K // P):
                 nc.vector.tensor_copy(dx[m][:].indirect(entries(list1, e * C1, C1)), results[e][:, m, :])

@@ -30,10 +30,7 @@ def tile_moe_seb_silu_kernel(tc, dy_words, dy_scales, w2t, w1t, a, gate1, gate2,
     nc = tc.nc
     with ExitStack() as ctx:
         keep = ctx.enter_context(tc.tile_pool(name="keep", bufs=1))
-        raws = ctx.enter_context(tc.tile_pool(name="raws", bufs=9))
-        ring = ctx.enter_context(tc.tile_pool(name="ring", bufs=3))
-        codes2 = ctx.enter_context(tc.tile_pool(name="codes2", bufs=6))
-        psum = ctx.enter_context(tc.psum_pool(name="psum", bufs=4))
+        psum = ctx.enter_context(tc.psum_pool(name="psum", bufs=1))
 
         list1 = keep.tile([P, T // LIST_ROWS], U16, name="list1")
         list2 = keep.tile([P, T // LIST_ROWS], U16, name="list2")
@@ -52,7 +49,7 @@ def tile_moe_seb_silu_kernel(tc, dy_words, dy_scales, w2t, w1t, a, gate1, gate2,
             return lst[:, first // LIST_ROWS : (first + count) // LIST_ROWS]
 
         def load_w2(f, s):
-            raw = raws.tile([P, PACK, H], F32, name="raw")
+            raw = keep.tile([P, PACK, H], F32, name=f"raw2_{(PASSES * f + s) % 10}", align_bytes=64)
             nc.sync.dma_start(out=raw[:], in_=w2t[f, s * K_PASS : (s + 1) * K_PASS, :].rearrange("(p j) c -> p j c", j=PACK))
             return raw
 
@@ -62,54 +59,55 @@ def tile_moe_seb_silu_kernel(tc, dy_words, dy_scales, w2t, w1t, a, gate1, gate2,
                 nc.sync.dma_start(out=dst[r:P:RUN, :, :], in_=rows[r])
 
         def load_w1(e):
-            raw = raws.tile([P, PACK, K], F32, name="raw")
+            raw = keep.tile([P, PACK, K], F32, name=f"raw1_{e}", align_bytes=64)
             load_hidden_rows(raw, w1t[e])
             return raw
 
         def quantize(pool, tag, grouped, width):
             codes = pool.tile([P, width], U32, name=tag + "_codes", align_bytes=64)
             scales = pool.tile([P, width], U8, name=tag + "_scales", align_bytes=64)
-            nc.vector.quantize_mx(out=codes[:].bitcast(FP8X4), scales=scales[:], in_=grouped[:])
+            nc.vector.quantize_mx(out=codes[:].bitcast(FP8X4), scales=scales[:], in_=grouped)
             return codes, scales
 
-        def group_w2(raw, on_vector):
-            grouped = ring.tile([P, PACK * H], BF16, name="grouped", align_bytes=64)
+        def grouped_tile(n):
+            return keep.tile([P, PACK * H], BF16, name=f"grouped{n % 4}", align_bytes=64)
+
+        def group_w2(raw, n, on_vector):
+            grouped = grouped_tile(n)
             dst = grouped[:].rearrange("p (t g r j) -> p g t j r", t=PACK, r=RUN, j=PACK)
             src = raw[:].rearrange("p j (g t r) -> p g t j r", t=PACK, r=RUN)
             if on_vector:
                 nc.vector.tensor_copy(out=dst, in_=src)
             else:
                 nc.scalar.copy(out=dst, in_=src)
-            return grouped
+            return grouped[:]
 
-        def group_plain(raw, width, tag):
-            grouped = ring.tile([P, PACK * width], BF16, name=tag, align_bytes=64)
+        def group_plain(raw, grouped):
             nc.scalar.copy(
-                out=grouped[:].rearrange("p (c r t) -> p c t r", r=RUN, t=PACK),
-                in_=raw[:].rearrange("p t (c r) -> p c t r", r=RUN),
+                out=grouped.rearrange("p (c r t) -> p c t r", r=RUN, t=PACK),
+                in_=raw.rearrange("p t (c r) -> p c t r", r=RUN),
             )
             return grouped
 
         warm = keep.tile([P, 2], F32, name="warm")
         nc.gpsimd.memset(warm[:, 0:1], 0.0)
-        nc.scalar.activation(out=warm[:, 1:2], in_=warm[:, 0:1], func=ACT.Silu)
-        nc.vector.memset(dy_in_scales[:].bitcast(I32), 0)
+        nc.scalar.activation(out=warm[:, 1:2], in_=warm[:, 0:1], func=ACT.Sigmoid)
+        nc.gpsimd.memset(dy_in_scales[:].bitcast(I32), 0)
+        a_rows = a.rearrange("(g t r) c -> t g r c", t=PACK, r=RUN)
         nc.sync.dma_start(list2[:], offs2)
-        for s in range(PASSES):
-            nc.sync.dma_start(out=dy_in[s][:], in_=dy_words[s].rearrange("p t d -> p (t d)").bitcast(I32))
-        raw2 = {(0, 0): load_w2(0, 0)}
+        for t in range(PACK):
+            if t < PASSES:
+                nc.sync.dma_start(out=dy_in[t][:], in_=dy_words[t].rearrange("p t d -> p (t d)").bitcast(I32))
+            nc.sync.dma_start(out=pre[:, t, :], in_=a_rows[t])
         for q in range(4):
             nc.sync.dma_start(
                 out=dy_in_scales[32 * q : 32 * q + 4 * PASSES, :].bitcast(I32),
                 in_=dy_scales[:, 4 * q : 4 * q + 4, :].bitcast(I32),
             )
-        raw2[0, 1] = load_w2(0, 1)
+        raw2 = {(f, s): load_w2(f, s) for f in range(2) for s in range(PASSES)}
         nc.sync.dma_start(out=g2[:], in_=gate2)
-        load_hidden_rows(pre, a)
         nc.sync.dma_start(out=g1[:], in_=gate1)
         nc.sync.dma_start(list1[:], offs)
-        for s in range(PASSES):
-            raw2[1, s] = load_w2(1, s)
 
         for first, count in ((0, GATHER2), (GATHER2, T - GATHER2)):
             cols = slice(first, first + count)
@@ -119,11 +117,11 @@ def tile_moe_seb_silu_kernel(tc, dy_words, dy_scales, w2t, w1t, a, gate1, gate2,
             nc.vector.tensor_copy(dy_slot_scales[:, cols], dy_in_scales[:].indirect(which))
 
         def second_weights(f):
-            return [quantize(codes2, "w2", group_w2(raw2[f, s], f == 1), H) for s in range(PASSES)]
+            return [quantize(keep, f"w2_{f % 2}_{s}", group_w2(raw2[f, s], PASSES * f + s, f == 0), H) for s in range(PASSES)]
 
         def second_layer(f, w):
             cols = slice(f * C2, (f + 1) * C2)
-            acc = psum.tile([P, PACK, C2], F32, name="acc2")
+            acc = psum.tile([P, PACK, C2], F32, name=f"acc2_{f % 3}")
             for t in range(PACK):
                 w_cols = slice(t * P, (t + 1) * P)
                 for s in range(PASSES):
@@ -146,22 +144,20 @@ def tile_moe_seb_silu_kernel(tc, dy_words, dy_scales, w2t, w1t, a, gate1, gate2,
                     dc[t][:].indirect(entries(list2, f * C2, C2)), sums[:, t, :], g2[:, cols], ALU.mult
                 )
 
-        def silu_parts():
+        def make_factor():
             for t in range(PACK):
-                nc.scalar.activation(out=factor[:, t, :], in_=pre[:, t, :], func=ACT.Silu, scale=-1.0)
-
-        def make_factor(e):
-            cols = slice(e * C1, (e + 1) * C1)
-            nc.scalar.activation(out=pre[:, :, cols], in_=pre[:, :, cols], func=ACT.Sigmoid)
-            nc.vector.scalar_tensor_tensor(
-                out=factor[:, :, cols], in0=factor[:, :, cols], scalar=1.0, in1=pre[:, :, cols],
-                op0=ALU.subtract, op1=ALU.mult,
-            )
-            nc.vector.scalar_tensor_tensor(
-                out=factor[:, :, cols], in0=factor[:, :, cols], scalar=-1.0,
-                in1=g1[:, cols].unsqueeze(1).to_broadcast([P, PACK, C1]),
-                op0=ALU.mult, op1=ALU.mult,
-            )
+                nc.scalar.activation(out=factor[:, t, :], in_=pre[:, t, :], func=ACT.Sigmoid)
+            for e in range(E1):
+                cols = slice(e * C1, (e + 1) * C1)
+                nc.scalar.activation(out=pre[:, :, cols], in_=pre[:, :, cols], func=ACT.Silu, scale=-1.0)
+                nc.vector.scalar_tensor_tensor(
+                    out=factor[:, :, cols], in0=pre[:, :, cols], scalar=1.0, in1=factor[:, :, cols],
+                    op0=ALU.subtract, op1=ALU.mult,
+                )
+            for t in range(PACK):
+                nc.vector.scalar_tensor_tensor(
+                    out=factor[:, t, :], in0=factor[:, t, :], scalar=-1.0, in1=g1[:], op0=ALU.mult, op1=ALU.mult
+                )
 
         raw1 = {}
         for f in range(E2):
@@ -169,37 +165,31 @@ def tile_moe_seb_silu_kernel(tc, dy_words, dy_scales, w2t, w1t, a, gate1, gate2,
                 for s in range(PASSES):
                     raw2[f + 2, s] = load_w2(f + 2, s)
             w = second_weights(f)
-            if f >= 2:
+            if f >= 1:
                 scatter_dc(f - 1, acc, raw2[f, 1][:, 0, :].rearrange("p (t c) -> p t c", t=PACK))
             acc = second_layer(f, w)
-            if f in (0, E2 - 1):
+            if f == E2 - 1:
                 scatter_dc(f, acc, keep.tile([P, PACK, C2], F32, name="sums2")[:])
             if f == 0:
-                silu_parts()
-            if f == 1:
-                for e in range(E1):
-                    make_factor(e)
+                make_factor()
         for e in range(E1):
             raw1[e] = load_w1(e)
-        w1q = [quantize(keep, f"w1_{e}", group_plain(raw1[e], K, "grouped"), K) for e in range(E1)]
+        w1q = [quantize(keep, f"w1_{e}", group_plain(raw1[e][:], grouped_tile(PASSES * E2 + e)[:]), K) for e in range(E1)]
 
-        def gather_da(e):
-            cols = slice(e * C1, (e + 1) * C1)
-            da = ring.tile([P, PACK, C1], F32, name="da")
+        def gather_da(first, count, da):
+            cols = slice(first, first + count)
             for t in range(PACK):
                 nc.vector.tensor_tensor(
-                    da[:, t, :], dc[t][:].indirect(entries(list1, e * C1, C1)), factor[:, t, cols], ALU.mult
+                    da[:, t, :], dc[t][:].indirect(entries(list1, first, count)), factor[:, t, cols], ALU.mult
                 )
-            return group_plain(da, C1, "da_grouped")
 
-        def first_layer(e, grouped):
-            da_codes, da_scales = quantize(ring, "da", grouped, C1)
+        def first_layer(e, da_codes, da_scales):
             if e + 1 < E1:
-                sums = raw1[e + 1][:, 0:2, :].rearrange("p j (u c) -> p (j u) c", c=C1)
+                sums = raw1[e + 1][:, 2:4, :].rearrange("p j (u c) -> p (j u) c", c=C1)
             else:
                 sums = keep.tile([P, K // P, C1], F32, name="sums1")[:]
             for half in range(2):
-                acc = psum.tile([P, 2, C1], F32, name="acc1")
+                acc = psum.tile([P, 2, C1], F32, name=f"acc1_{(2 * e + half) % 4}")
                 for u in range(2):
                     m = 2 * half + u
                     w_cols = slice(m * P, (m + 1) * P)
@@ -215,12 +205,19 @@ def tile_moe_seb_silu_kernel(tc, dy_words, dy_scales, w2t, w1t, a, gate1, gate2,
                 nc.scalar.copy(out=sums[:, 2 * half : 2 * half + 2, :], in_=acc[:])
             return sums
 
-        groups = [gather_da(0)]
-        results = []
-        for e in range(E1):
-            if e + 1 < E1:
-                groups.append(gather_da(e + 1))
-            results.append(first_layer(e, groups[e]))
+        last = E1 - 1
+        da_early = keep.tile([P, PACK, last * C1], F32, name="da_early")
+        gather_da(0, last * C1, da_early)
+        daq = []
+        for e in range(last):
+            grouped = group_plain(da_early[:, :, e * C1 : (e + 1) * C1], raw1[last][:, 2 + e, :].bitcast(BF16))
+            daq.append(quantize(keep, f"da{e}", grouped, C1))
+        results = [first_layer(0, *daq[0])]
+        da_last = raw1[last][:, 2:4, :].rearrange("p j (u c) -> p (j u) c", c=C1)
+        gather_da(last * C1, C1, da_last)
+        grouped = keep.tile([P, PACK * C1], BF16, name="da_grouped", align_bytes=64)
+        daq.append(quantize(keep, f"da{last}", group_plain(da_last, grouped[:]), C1))
+        results.extend(first_layer(e, *daq[e]) for e in range(1, E1))
         for e in range(E1):
             for m in range(K // P):
                 nc.vector.tensor_copy(dx[m][:].indirect(entries(list1, e * C1, C1)), results[e][:, m, :])

@@ -90,23 +90,23 @@ def tile_moe_seb_silu_kernel(tc, dy_words, dy_scales, w2t, w1t, a, gate1, gate2,
             return grouped
 
         warm = keep.tile([P, 2], F32, name="warm")
+        nc.gpsimd.memset(dy_in_scales[:].bitcast(I32), 0)
         nc.gpsimd.memset(warm[:, 0:1], 0.0)
         nc.scalar.activation(out=warm[:, 1:2], in_=warm[:, 0:1], func=ACT.Sigmoid)
-        nc.gpsimd.memset(dy_in_scales[:].bitcast(I32), 0)
         a_rows = a.rearrange("(g t r) c -> t g r c", t=PACK, r=RUN)
         nc.sync.dma_start(list2[:], offs2)
-        for t in range(PACK):
-            if t < PASSES:
-                nc.sync.dma_start(out=dy_in[t][:], in_=dy_words[t].rearrange("p t d -> p (t d)").bitcast(I32))
-            nc.sync.dma_start(out=pre[:, t, :], in_=a_rows[t])
         for q in range(4):
             nc.sync.dma_start(
                 out=dy_in_scales[32 * q : 32 * q + 4 * PASSES, :].bitcast(I32),
                 in_=dy_scales[:, 4 * q : 4 * q + 4, :].bitcast(I32),
             )
+        for t in range(PACK):
+            if t < PASSES:
+                nc.sync.dma_start(out=dy_in[t][:], in_=dy_words[t].rearrange("p t d -> p (t d)").bitcast(I32))
+            nc.sync.dma_start(out=pre[:, t, :], in_=a_rows[t])
+        nc.sync.dma_start(out=g1[:], in_=gate1)
         raw2 = {(f, s): load_w2(f, s) for f in range(2) for s in range(PASSES)}
         nc.sync.dma_start(out=g2[:], in_=gate2)
-        nc.sync.dma_start(out=g1[:], in_=gate1)
         nc.sync.dma_start(list1[:], offs)
 
         for first, count in ((0, GATHER2), (GATHER2, T - GATHER2)):
@@ -117,7 +117,7 @@ def tile_moe_seb_silu_kernel(tc, dy_words, dy_scales, w2t, w1t, a, gate1, gate2,
             nc.vector.tensor_copy(dy_slot_scales[:, cols], dy_in_scales[:].indirect(which))
 
         def second_weights(f):
-            return [quantize(keep, f"w2_{f % 2}_{s}", group_w2(raw2[f, s], PASSES * f + s, f == 0), H) for s in range(PASSES)]
+            return [quantize(keep, f"w2_{f % 2}_{s}", group_w2(raw2[f, s], PASSES * f + s, f == 0 or (f, s) == (E2 // 2, 0)), H) for s in range(PASSES)]
 
         def second_layer(f, w):
             cols = slice(f * C2, (f + 1) * C2)
@@ -147,16 +147,15 @@ def tile_moe_seb_silu_kernel(tc, dy_words, dy_scales, w2t, w1t, a, gate1, gate2,
         def make_factor():
             for t in range(PACK):
                 nc.scalar.activation(out=factor[:, t, :], in_=pre[:, t, :], func=ACT.Sigmoid)
+                nc.vector.scalar_tensor_tensor(
+                    out=factor[:, t, :], in0=factor[:, t, :], scalar=-1.0, in1=g1[:], op0=ALU.mult, op1=ALU.mult
+                )
             for e in range(E1):
                 cols = slice(e * C1, (e + 1) * C1)
                 nc.scalar.activation(out=pre[:, :, cols], in_=pre[:, :, cols], func=ACT.Silu, scale=-1.0)
                 nc.vector.scalar_tensor_tensor(
                     out=factor[:, :, cols], in0=pre[:, :, cols], scalar=1.0, in1=factor[:, :, cols],
                     op0=ALU.subtract, op1=ALU.mult,
-                )
-            for t in range(PACK):
-                nc.vector.scalar_tensor_tensor(
-                    out=factor[:, t, :], in0=factor[:, t, :], scalar=-1.0, in1=g1[:], op0=ALU.mult, op1=ALU.mult
                 )
 
         raw1 = {}

from contextlib import ExitStack

import concourse.mybir as mybir

K, T, H, N = 512, 768, 512, 1024
E1, C1 = 3, 256
E2, C2 = 6, 128
FLOPS = 2 * T * (N * H + H * K)

F32 = mybir.dt.float32
BF16 = mybir.dt.bfloat16
I32 = mybir.dt.int32
U32 = mybir.dt.uint32
U16 = mybir.dt.uint16
U8 = mybir.dt.uint8
FP8X4 = mybir.dt.float8_e4m3fn_x4
ACT = mybir.ActivationFunctionType
ALU = mybir.AluOpType

P = 128
PACK = 4
K_PASS = P * PACK
PASSES = N // K_PASS
RUN = 2
LIST_ROWS = 16
GATHER2 = 256


def tile_moe_seb_silu_kernel(tc, dy_words, dy_scales, w2t, w1t, a, gate1, gate2, offs, offs2, out):
    nc = tc.nc
    with ExitStack() as ctx:
        keep = ctx.enter_context(tc.tile_pool(name="keep", bufs=1))
        psum = ctx.enter_context(tc.psum_pool(name="psum", bufs=1))

        list1 = keep.tile([P, T // LIST_ROWS], U16, name="list1")
        list2 = keep.tile([P, T // LIST_ROWS], U16, name="list2")
        dy_in = [keep.tile([P, T], I32, name=f"dy_in{s}", align_bytes=64) for s in range(PASSES)]
        dy_in_scales = keep.tile([P, T], U8, name="dy_in_scales", align_bytes=64)
        dy_slots = [keep.tile([P, T], U32, name=f"dy_slots{s}", align_bytes=64) for s in range(PASSES)]
        dy_slot_scales = keep.tile([P, T], U8, name="dy_slot_scales", align_bytes=64)
        g1 = keep.tile([P, T], F32, name="g1")
        g2 = keep.tile([P, T], F32, name="g2")
        pre = keep.tile([P, PACK, T], F32, name="pre")
        factor = keep.tile([P, PACK, T], F32, name="factor")
        dc = [keep.tile([P, T], F32, name=f"dc{t}") for t in range(PACK)]
        dx = [keep.tile([P, T], F32, name=f"dx{m}") for m in range(K // P)]

        def entries(lst, first, count):
            return lst[:, first // LIST_ROWS : (first + count) // LIST_ROWS]

        def load_w2(f, s):
            raw = keep.tile([P, PACK, H], F32, name=f"raw2_{(PASSES * f + s) % 10}", align_bytes=64)
            nc.sync.dma_start(out=raw[:], in_=w2t[f, s * K_PASS : (s + 1) * K_PASS, :].rearrange("(p j) c -> p j c", j=PACK))
            return raw

        def load_hidden_rows(dst, src):
            rows = src.rearrange("(g t r) c -> r g t c", t=PACK, r=RUN)
            for r in range(RUN):
                nc.sync.dma_start(out=dst[r:P:RUN, :, :], in_=rows[r])

        def load_w1(e):
            raw = keep.tile([P, PACK, K], F32, name=f"raw1_{e}", align_bytes=64)
            load_hidden_rows(raw, w1t[e])
            return raw

        def quantize(pool, tag, grouped, width):
            codes = pool.tile([P, width], U32, name=tag + "_codes", align_bytes=64)
            scales = pool.tile([P, width], U8, name=tag + "_scales", align_bytes=64)
            nc.vector.quantize_mx(out=codes[:].bitcast(FP8X4), scales=scales[:], in_=grouped)
            return codes, scales

        def grouped_tile(n):
            return keep.tile([P, PACK * H], BF16, name=f"grouped{n % 4}", align_bytes=64)

        def group_w2(raw, n, on_vector):
            grouped = grouped_tile(n)
            dst = grouped[:].rearrange("p (t g r j) -> p g t j r", t=PACK, r=RUN, j=PACK)
            src = raw[:].rearrange("p j (g t r) -> p g t j r", t=PACK, r=RUN)
            if on_vector:
                nc.vector.tensor_copy(out=dst, in_=src)
            else:
                nc.scalar.copy(out=dst, in_=src)
            return grouped[:]

        def group_plain(raw, grouped):
            nc.scalar.copy(
                out=grouped.rearrange("p (c r t) -> p c t r", r=RUN, t=PACK),
                in_=raw.rearrange("p t (c r) -> p c t r", r=RUN),
            )
            return grouped

        warm = keep.tile([P, 2], F32, name="warm")
        nc.gpsimd.memset(dy_in_scales[:].bitcast(I32), 0)
        nc.gpsimd.memset(warm[:, 0:1], 0.0)
        nc.scalar.activation(out=warm[:, 1:2], in_=warm[:, 0:1], func=ACT.Sigmoid)
        a_rows = a.rearrange("(g t r) c -> t g r c", t=PACK, r=RUN)
        nc.sync.dma_start(list2[:], offs2)
        for q in range(4):
            nc.sync.dma_start(
                out=dy_in_scales[32 * q : 32 * q + 4 * PASSES, :].bitcast(I32),
                in_=dy_scales[:, 4 * q : 4 * q + 4, :].bitcast(I32),
            )
        for t in range(PACK):
            if t < PASSES:
                nc.sync.dma_start(out=dy_in[t][:], in_=dy_words[t].rearrange("p t d -> p (t d)").bitcast(I32))
            nc.sync.dma_start(out=pre[:, t, :], in_=a_rows[t])
        nc.sync.dma_start(out=g1[:], in_=gate1)
        raw2 = {(f, s): load_w2(f, s) for f in range(2) for s in range(PASSES)}
        nc.sync.dma_start(out=g2[:], in_=gate2)
        nc.sync.dma_start(list1[:], offs)

        for first, count in ((0, GATHER2), (GATHER2, T - GATHER2)):
            cols = slice(first, first + count)
            which = entries(list2, first, count)
            for s in range(PASSES):
                nc.vector.tensor_copy(dy_slots[s][:, cols], dy_in[s][:].bitcast(U32).indirect(which))
            nc.vector.tensor_copy(dy_slot_scales[:, cols], dy_in_scales[:].indirect(which))

        def second_weights(f):
            return [quantize(keep, f"w2_{f % 2}_{s}", group_w2(raw2[f, s], PASSES * f + s, f == 0 or (f, s) == (E2 // 2, 0)), H) for s in range(PASSES)]

        def second_layer(f, w):
            cols = slice(f * C2, (f + 1) * C2)
            acc = psum.tile([P, PACK, C2], F32, name=f"acc2_{f % 3}")
            for t in range(PACK):
                w_cols = slice(t * P, (t + 1) * P)
                for s in range(PASSES):
                    nc.tensor.matmul_mx(
                        out=acc[:, t, :],
                        lhsT=w[s][0][:, w_cols].bitcast(FP8X4),
                        lhsT_scale=w[s][1][:, w_cols],
                        rhs=dy_slots[s][:, cols].bitcast(FP8X4),
                        rhs_scale=dy_slot_scales[4 * s : P, cols],
                        start=(s == 0),
                        stop=(s == PASSES - 1),
                    )
            return acc

        def scatter_dc(f, acc, sums):
            cols = slice(f * C2, (f + 1) * C2)
            nc.scalar.copy(out=sums, in_=acc[:])
            for t in range(PACK):
                nc.vector.tensor_tensor(
                    dc[t][:].indirect(entries(list2, f * C2, C2)), sums[:, t, :], g2[:, cols], ALU.mult
                )

        def make_factor():
            for t in range(PACK):
                nc.scalar.activation(out=factor[:, t, :], in_=pre[:, t, :], func=ACT.Sigmoid)
                nc.vector.scalar_tensor_tensor(
                    out=factor[:, t, :], in0=factor[:, t, :], scalar=-1.0, in1=g1[:], op0=ALU.mult, op1=ALU.mult
                )
            for e in range(E1):
                cols = slice(e * C1, (e + 1) * C1)
                nc.scalar.activation(out=pre[:, :, cols], in_=pre[:, :, cols], func=ACT.Silu, scale=-1.0)
                nc.vector.scalar_tensor_tensor(
                    out=factor[:, :, cols], in0=pre[:, :, cols], scalar=1.0, in1=factor[:, :, cols],
                    op0=ALU.subtract, op1=ALU.mult,
                )

        raw1 = {}
        for f in range(E2):
            if f + 2 < E2:
                for s in range(PASSES):
                    raw2[f + 2, s] = load_w2(f + 2, s)
            w = second_weights(f)
            if f >= 1:
                scatter_dc(f - 1, acc, raw2[f, 1][:, 0, :].rearrange("p (t c) -> p t c", t=PACK))
            acc = second_layer(f, w)
            if f == E2 - 1:
                scatter_dc(f, acc, keep.tile([P, PACK, C2], F32, name="sums2")[:])
            if f == 0:
                make_factor()
        for e in range(E1):
            raw1[e] = load_w1(e)
        w1q = [quantize(keep, f"w1_{e}", group_plain(raw1[e][:], grouped_tile(PASSES * E2 + e)[:]), K) for e in range(E1)]

        def gather_da(first, count, da):
            cols = slice(first, first + count)
            for t in range(PACK):
                nc.vector.tensor_tensor(
                    da[:, t, :], dc[t][:].indirect(entries(list1, first, count)), factor[:, t, cols], ALU.mult
                )

        def first_layer(e, da_codes, da_scales):
            if e + 1 < E1:
                sums = raw1[e + 1][:, 2:4, :].rearrange("p j (u c) -> p (j u) c", c=C1)
            else:
                sums = keep.tile([P, K // P, C1], F32, name="sums1")[:]
            for half in range(2):
                acc = psum.tile([P, 2, C1], F32, name=f"acc1_{(2 * e + half) % 4}")
                for u in range(2):
                    m = 2 * half + u
                    w_cols = slice(m * P, (m + 1) * P)
                    nc.tensor.matmul_mx(
                        out=acc[:, u, :],
                        lhsT=w1q[e][0][:, w_cols].bitcast(FP8X4),
                        lhsT_scale=w1q[e][1][:, w_cols],
                        rhs=da_codes[:].bitcast(FP8X4),
                        rhs_scale=da_scales[:],
                        start=True,
                        stop=True,
                    )
                nc.scalar.copy(out=sums[:, 2 * half : 2 * half + 2, :], in_=acc[:])
            return sums

        last = E1 - 1
        da_early = keep.tile([P, PACK, last * C1], F32, name="da_early")
        gather_da(0, last * C1, da_early)
        daq = []
        for e in range(last):
            grouped = group_plain(da_early[:, :, e * C1 : (e + 1) * C1], raw1[last][:, 2 + e, :].bitcast(BF16))
            daq.append(quantize(keep, f"da{e}", grouped, C1))
        results = [first_layer(0, *daq[0])]
        da_last = raw1[last][:, 2:4, :].rearrange("p j (u c) -> p (j u) c", c=C1)
        gather_da(last * C1, C1, da_last)
        grouped = keep.tile([P, PACK * C1], BF16, name="da_grouped", align_bytes=64)
        daq.append(quantize(keep, f"da{last}", group_plain(da_last, grouped[:]), C1))
        results.extend(first_layer(e, *daq[e]) for e in range(1, E1))
        for e in range(E1):
            for m in range(K // P):
                nc.vector.tensor_copy(dx[m][:].indirect(entries(list1, e * C1, C1)), results[e][:, m, :])
        for m in range(K // P):
            nc.sync.dma_start(out=out[m * P : (m + 1) * P, :], in_=dx[m][:])
